import numpy as np
import ml_dtypes


def mxq(x, axis, fmt="e4m3"):
    dtype, down = {"e4m3": (ml_dtypes.float8_e4m3fn, 7), "e5m2": (ml_dtypes.float8_e5m2, 14)}[fmt]
    v = np.moveaxis(np.asarray(x, np.float32).astype(ml_dtypes.bfloat16).astype(np.float64), axis, -1)
    blocks = v.reshape(v.shape[:-1] + (-1, 32))
    amax = np.abs(blocks).max(-1, keepdims=True)
    byte = np.maximum(np.where(amax > 0, np.frexp(amax)[1] - 1 + 127, 0) - down, 1)
    scale = np.exp2(byte - 127.0)
    codes = (blocks / scale).astype(np.float32).astype(dtype).astype(np.float64)
    return np.moveaxis((codes * scale).reshape(v.shape), -1, axis)


WIDE = False


def mx_kscale(k):
    if not WIDE:
        return np.ones(k)
    levels = np.array([10, -10, 5, -5, 0])
    if k % 512:
        return np.exp2(np.random.permutation(np.resize(levels, k // 32))).repeat(32)
    a = np.empty((k // 512, 16))
    for p in range(k // 512):
        a[p, :8] = np.random.permutation(np.resize(levels, 8))
        for g in range(8):
            far = levels[np.abs(levels - a[p, g]) >= 10]
            a[p, g + 8] = far[np.random.randint(len(far))]
    return np.exp2(a.ravel()).repeat(32)


def f64(x):
    return np.asarray(x).astype(np.float64)


def striped(idx):
    return np.tile(idx.reshape(-1, 16).T, (8, 1)).astype(np.uint16)


def unstriped(offs):
    return offs[:16].T.reshape(-1).astype(np.int64)


E2M1 = np.array([0.0, 0.5, 1.0, 1.5, 2.0, 3.0, 4.0, 6.0, -0.0, -0.5, -1.0, -1.5, -2.0, -3.0, -4.0, -6.0])


def pack_weight(w, fmt):
    k, n = w.shape
    w = f64(np.asarray(w, np.float32).astype(ml_dtypes.bfloat16)).reshape(k // 32, 32, n)
    amax = np.abs(w).max(1)
    if fmt == "e4m3":
        byte = np.frexp(amax)[1] - 1 + 127 - 7
    else:
        mant, ex = np.frexp(amax / 6.0)
        byte = np.where(mant > 0.5, ex, ex - 1) + 127
    byte = np.clip(np.where(amax > 0, byte, 1), 1, 254)
    scaled = (w * np.exp2(127.0 - byte)[:, None, :]).reshape(k, n).astype(np.float32)
    by_word = np.ascontiguousarray(scaled.reshape(k // 512, 128, 4, n).transpose(0, 1, 3, 2))
    if fmt == "e4m3":
        words = by_word.astype(ml_dtypes.float8_e4m3fn).view(np.uint8)
    else:
        c = by_word.astype(ml_dtypes.float4_e2m1fn).view(np.uint8) & 0xF
        words = (c[..., 0::2] | (c[..., 1::2] << 4)).reshape(k // 512, 128, 2 * n)
    return np.ascontiguousarray(words), np.ascontiguousarray(byte.astype(np.uint8).reshape(k // 512, 16, n))


def unpack_weight(words, scales, fmt):
    g, _, n = scales.shape
    words = np.ascontiguousarray(words).reshape(g, 128, n, -1)
    if fmt == "e4m3":
        vals = words.view(ml_dtypes.float8_e4m3fn).astype(np.float64)
    else:
        nib = np.empty((g, 128, n, 4), np.uint8)
        nib[..., 0::2] = words & 0xF
        nib[..., 1::2] = words >> 4
        vals = E2M1[nib]
    vals = vals * np.repeat(np.exp2(scales.astype(np.float64) - 127.0), 8, axis=1)[..., None]
    return vals.transpose(0, 1, 3, 2).reshape(g * 512, n)


def gelu(v):
    return 0.5 * v * (1.0 + np.tanh(np.sqrt(2.0 / np.pi) * (v + 0.044715 * v**3)))


def often(T, S):
    return np.random.permutation(T)[(T * np.random.uniform(0, 1, S) ** 4).astype(np.int64)]


K, K2, T, S, P, H = 1024, 512, 4096, 1024, 512, 512


def setup_inputs():
    n = np.random.standard_normal
    s, s2, s3 = mx_kscale(K)[:, None], mx_kscale(K2)[:, None], mx_kscale(K)[:, None]
    u = mx_kscale(H)[:, None]
    inp = {}
    inp["tab_words"], inp["tab_scales"] = pack_weight(n((K, T)) * s, "e4m3")
    inp["tab2_words"], inp["tab2_scales"] = pack_weight(n((K2, T)) * s2, "e4m3")
    inp["tab3_words"], inp["tab3_scales"] = pack_weight(n((K, T)) * s3, "e4m3")
    inp["offs"] = striped(np.random.permutation(T)[:S])
    inp["offs2"] = striped(np.random.permutation(T)[:S])
    inp["offs3"] = striped(np.random.permutation(T)[:S])
    inp["pos1"] = striped(np.random.permutation(S)[:P])
    inp["pos2"] = striped(often(S, P))
    inp["pos3"] = striped(often(S, P))
    inp["w1"] = (n((K, H)) / s / K ** 0.5).astype(np.float32)
    inp["w2_words"], inp["w2_scales"] = pack_weight(n((K2, H)) / s2 / K2 ** 0.5, "e2m1")
    inp["w3"] = (n((K, H)) / s3 / K ** 0.5).astype(np.float32)
    inp["gain"] = (np.exp(0.3 * n(H)) * u[:, 0]).astype(np.float32)
    inp["w4_words"], inp["w4_scales"] = pack_weight(n((H, H)) / u / H ** 0.5, "e4m3")
    return inp


def reference(tab_words, tab_scales, tab2_words, tab2_scales, tab3_words, tab3_scales, offs, offs2, offs3,
              pos1, pos2, pos3, w1, w2_words, w2_scales, w3, gain, w4_words, w4_scales):
    v = unpack_weight(tab_words, tab_scales, "e4m3")[:, unstriped(offs)]
    v2 = unpack_weight(tab2_words, tab2_scales, "e4m3")[:, unstriped(offs2)]
    v3 = unpack_weight(tab3_words, tab3_scales, "e4m3")[:, unstriped(offs3)]
    a = mxq(f64(w1), 0, "e4m3").T @ v
    b = unpack_weight(w2_words, w2_scales, "e2m1").T @ v2
    d = mxq(f64(w3), 0, "e4m3").T @ v3
    join = np.tanh(np.maximum(a[:, unstriped(pos1)], b[:, unstriped(pos2)]) - d[:, unstriped(pos3)])
    z = f64(gain)[:, None] * join
    y = unpack_weight(w4_words, w4_scales, "e4m3").T @ mxq(z, 0, "e4m3")
    return y + join

@@ -1,0 +1,302 @@
+from contextlib import ExitStack
+
+import concourse.mybir as mybir
+
+F32 = mybir.dt.float32
+BF16 = mybir.dt.bfloat16
+I32 = mybir.dt.int32
+U32 = mybir.dt.uint32
+U16 = mybir.dt.uint16
+U8 = mybir.dt.uint8
+FP8X4 = mybir.dt.float8_e4m3fn_x4
+FP4X4 = mybir.dt.float4_e2m1fn_x4
+ACT = mybir.ActivationFunctionType
+ALU = mybir.AluOpType
+
+P = 128
+T = 4096
+S = 1024
+J = 512
+H = 512
+N = 512
+FLOPS = 2952790016
+
+
+def tile_list_haulage_permit_join_kernel(
+    tc, tab_words, tab_scales, tab2_words, tab2_scales, tab3_words, tab3_scales, offs, offs2, offs3,
+    pos1, pos2, pos3, w1, w2_words, w2_scales, w3, gain, w4_words, w4_scales, out,
+):
+    nc = tc.nc
+    with ExitStack() as ctx:
+        keep = ctx.enter_context(tc.tile_pool(name="keep", bufs=1))
+        psum = ctx.enter_context(tc.psum_pool(name="psum", bufs=1))
+
+        def tile(shape, dtype, name, tag=None):
+            return keep.tile(shape, dtype, name=name, tag=tag or name, align_bytes=64)
+
+        def load_list(src, name):
+            lst = keep.tile(list(src.shape), U16, name=name)
+            nc.sync.dma_start(lst[:], src)
+            return lst
+
+        def words_view(words, a):
+            return words[a].rearrange("p n t -> p (n t)").bitcast(I32)
+
+        def zeroed_plane(width, name, tag=None):
+            plane = tile([P, width], U8, name, tag)
+            nc.vector.memset(plane[:].bitcast(I32), 0)
+            return plane
+
+        def load_scales(queue, plane, scales):
+            passes = scales.shape[0]
+            for q in range(4):
+                queue.dma_start(
+                    out=plane[32 * q : 32 * q + 4 * passes, :].bitcast(I32),
+                    in_=scales[:, 4 * q : 4 * q + 4, :].bitcast(I32),
+                )
+
+        def load_table(words, a, name, tag=None):
+            table = tile([P, T], I32, name, tag)
+            nc.sync.dma_start(out=table[:], in_=words_view(words, a))
+            return table
+
+        def load_weight(w, a, name, tag):
+            raw = tile([P, 4, H], F32, name, tag)
+            nc.sync.dma_start(out=raw[:], in_=w[512 * a : 512 * (a + 1), :].rearrange("(p j) c -> p j c", j=4))
+            return raw
+
+        def load_scale_rows(scales, name, tag):
+            rows = tile([P, T], U8, name, tag)
+            nc.vector.memset(rows[0:96, :].bitcast(I32), 0)
+            nc.sync.dma_start(
+                out=rows[96:P, :].bitcast(I32), in_=scales.rearrange("a q n -> (a q) n").bitcast(I32)
+            )
+            return rows
+
+        def gather_scales(rows, lst, name):
+            picked = tile([P, lst.shape[1] * 16], U8, name)
+            nc.vector.tensor_copy(picked[:], rows[:].indirect(lst))
+            return picked
+
+        def place_scale_rows(picked, plane, first_move, last_move):
+            for a, q in [divmod(i, 4) for i in range(first_move, last_move)]:
+                first = 96 + 16 * a + 4 * q
+                nc.sync.dma_start(
+                    out=plane[32 * q + 4 * a : 32 * q + 4 * a + 4, :].bitcast(I32),
+                    in_=picked[first : first + 4, :].bitcast(I32),
+                )
+
+        def gather_words(table, lst, name):
+            picked = tile([P, lst.shape[1] * 16], U32, name)
+            nc.vector.tensor_copy(picked[:], table[:].bitcast(U32).indirect(lst))
+            return picked
+
+        def half(lst, h):
+            columns = lst.shape[1] // 2
+            return lst[:, h * columns : (h + 1) * columns]
+
+        def halves(picked):
+            return [picked[:, h * N : (h + 1) * N] for h in range(2)]
+
+        def quantise_weight(raw, name, tag):
+            rounded = tile([P, 4 * H], BF16, name + "_bf", tag)
+            nc.scalar.activation(
+                out=rounded[:].rearrange("p (t m j) -> p m t j", t=4, j=4),
+                in_=raw[:].rearrange("p j (m t) -> p m t j", t=4),
+                func=ACT.Copy,
+            )
+            codes = tile([P, H], U32, name + "_codes")
+            plane = tile([P, H], U8, name + "_plane")
+            nc.vector.quantize_mx(out=codes[:].bitcast(FP8X4), scales=plane[:], in_=rounded[:])
+            return codes, plane
+
+        def bank(i, name):
+            return psum.tile([P, N], F32, name=name, tag="bank%d" % i)
+
+        def fp8_cols(codes, t):
+            return codes[:, t * P : (t + 1) * P].bitcast(FP8X4)
+
+        s2 = zeroed_plane(T, "s2", "raw2")
+        w2s = zeroed_plane(H, "w2s")
+        l1 = load_list(offs, "l1")
+        s1 = load_scale_rows(tab_scales, "s1", "raw1")
+        l3 = load_list(offs3, "l3")
+        s3 = load_scale_rows(tab3_scales, "s3", "tabB")
+        g1s = zeroed_plane(S, "g1s")
+        g3s = zeroed_plane(S, "g3s")
+        w2raw = tile([P, 2 * H], U8, "w2raw")
+        nc.sync.dma_start(out=w2raw[:].bitcast(I32), in_=w2_words[0].bitcast(I32))
+        l2 = load_list(offs2, "l2")
+        t2 = tile([P, T], I32, "t2", "tabA")
+        nc.sync.dma_start(out=t2[:, 0:2048], in_=words_view(tab2_words, 0)[:, 0:2048])
+        p1 = load_list(pos1, "p1")
+        p2 = load_list(pos2, "p2")
+        p3 = load_list(pos3, "p3")
+        nc.sync.dma_start(out=t2[:, 2048:T], in_=words_view(tab2_words, 0)[:, 2048:T])
+        load_scales(nc.sync, s2, tab2_scales)
+        w1raw0 = load_weight(w1, 0, "w1raw0", "raw0")
+        load_scales(nc.sync, w2s, w2_scales)
+
+        r1s = gather_scales(s1, l1[:], "r1s")
+        r3s = gather_scales(s3, l3[:], "r3s")
+        w2d = tile([P, 2 * H], U8, "w2d")
+        nc.vector.tensor_copy(
+            w2d[:].rearrange("p (t q b) -> p t q b", t=4, b=2),
+            w2raw[:].rearrange("p (q t b) -> p t q b", t=4, b=2),
+        )
+        place_scale_rows(r1s, g1s, 0, 2)
+        w1raw1 = load_weight(w1, 1, "w1raw1", "raw1")
+        place_scale_rows(r1s, g1s, 2, 8)
+        t10 = load_table(tab_words, 0, "t10", "tabB")
+        place_scale_rows(r3s, g3s, 0, 6)
+        w2sd = tile([P, H], U8, "w2sd")
+        nc.vector.tensor_copy(
+            w2sd[:].rearrange("p (t q) -> p t q", t=4), w2s[:].rearrange("p (q t) -> p t q", t=4)
+        )
+        g2s, g2 = [], []
+        for h in range(2):
+            g2s.append(gather_scales(s2, half(l2, h), "g2s%d" % h))
+            g2.append(gather_words(t2, half(l2, h), "g2%d" % h))
+        w3raw0 = load_weight(w3, 0, "w3raw0", "raw2")
+        place_scale_rows(r3s, g3s, 6, 8)
+        t11 = load_table(tab_words, 1, "t11", "tabA")
+        w1q0 = quantise_weight(w1raw0, "w1q0", "bf0")
+
+        order = [(t, h) for h in range(2) for t in range(4)]
+        bwin = [tile([P, S], F32, "bwin%d" % t) for t in range(4)]
+        for t, h in order:
+                acc = bank(2 * t + h, "b%d%d" % (t, h))
+                nc.tensor.matmul_mx(
+                    out=acc[:],
+                    lhsT=w2d[:, 2 * t * P : 2 * (t + 1) * P].bitcast(FP4X4),
+                    lhsT_scale=w2sd[:, t * P : (t + 1) * P],
+                    rhs=g2[h][:].bitcast(FP8X4),
+                    rhs_scale=g2s[h][:],
+                    start=True,
+                    stop=True,
+                )
+                nc.scalar.copy(out=bwin[t][:, h * N : (h + 1) * N], in_=acc[:])
+
+        w1q = [w1q0, quantise_weight(w1raw1, "w1q1", "bf1")]
+        w3raw1 = load_weight(w3, 1, "w3raw1", "raw0")
+
+        top = tile([P, 4, J], F32, "top")
+        for t in range(4):
+            nc.vector.tensor_copy(top[:, t, :], bwin[t][:].indirect(p2[:]))
+
+        def mx_pass(accs, order, wq, picked, picked_scales, a):
+            codes, plane = wq
+            for t, h in order:
+                nc.tensor.matmul_mx(
+                    out=accs[t, h][:],
+                    lhsT=fp8_cols(codes, t),
+                    lhsT_scale=plane[:, t * P : (t + 1) * P],
+                    rhs=picked[h].bitcast(FP8X4),
+                    rhs_scale=picked_scales[4 * a : P, h * N : (h + 1) * N],
+                    start=(a == 0),
+                    stop=(a == 1),
+                )
+
+        by_slice = [(t, h) for t in range(4) for h in range(2)]
+        g10 = halves(gather_words(t10, l1[:], "g10"))
+        t30 = load_table(tab3_words, 0, "t30", "tabB")
+        w3q0 = quantise_weight(w3raw0, "w3q0", "bf0")
+        w4raw = tile([P, H], I32, "w4raw", "g21")
+        nc.sync.dma_start(out=w4raw[:], in_=words_view(w4_words, 0))
+        load_scales(nc.sync, w2s, w4_scales)
+        g11 = [gather_words(t11, half(l1, h), "g11%d" % h)[:] for h in range(2)]
+        t31 = load_table(tab3_words, 1, "t31", "tabA")
+        accs = {(t, h): bank(2 * t + h, "a%d%d" % (t, h)) for t, h in by_slice}
+        mx_pass(accs, by_slice, w1q[0], g10, g1s, 0)
+        mx_pass(accs, order, w1q[1], g11, g1s, 1)
+        awin = [tile([P, S], F32, "awin%d" % t) for t in range(4)]
+        for t, h in order:
+            nc.scalar.copy(out=awin[t][:, h * N : (h + 1) * N], in_=accs[t, h][:])
+
+        w4d = tile([P, H], I32, "w4d", "g110")
+        nc.vector.tensor_copy(
+            w4d[:].rearrange("p (t q) -> p t q", t=4), w4raw[:].rearrange("p (q t) -> p t q", t=4)
+        )
+        w4sd = tile([P, H], U8, "w4sd", "g111")
+        nc.vector.tensor_copy(
+            w4sd[:].rearrange("p (t q) -> p t q", t=4), w2s[:].rearrange("p (q t) -> p t q", t=4)
+        )
+
+        w3q = [w3q0, quantise_weight(w3raw1, "w3q1", "bf1")]
+        gain_sb = tile([P, 4], F32, "gain_sb", "g10")
+        nc.sync.dma_start(out=gain_sb[:], in_=gain.rearrange("(p t) -> p t", t=4))
+        ga = tile([P, 4, J], F32, "ga")
+        for u in range(2):
+            for t in (2 * u, 2 * u + 1):
+                nc.vector.tensor_copy(ga[:, t, :], awin[t][:].indirect(p1[:]))
+            nc.vector.tensor_tensor(
+                out=top[:, 2 * u : 2 * u + 2, :], in0=ga[:, 2 * u : 2 * u + 2, :],
+                in1=top[:, 2 * u : 2 * u + 2, :], op=ALU.max,
+            )
+
+        g30 = halves(gather_words(t30, l3[:], "g30"))
+        accs = {(t, h): bank(2 * t + h, "d%d%d" % (t, h)) for t, h in by_slice}
+        mx_pass(accs, by_slice, w3q[0], g30, g3s, 0)
+        g31 = [gather_words(t31, half(l3, h), "g31%d" % h)[:] for h in range(2)]
+        mx_pass(accs, order, w3q[1], g31, g3s, 1)
+        dwin = [tile([P, S], F32, "dwin%d" % t, "bwin%d" % t) for t in range(4)]
+        for t, h in order:
+            if (t, h) in ((2, 0), (3, 0)):
+                nc.vector.tensor_copy(dwin[t][:, h * N : (h + 1) * N], accs[t, h][:])
+            else:
+                nc.scalar.copy(out=dwin[t][:, h * N : (h + 1) * N], in_=accs[t, h][:])
+
+        join = tile([P, 4, J], F32, "join")
+        z = tile([P, 4, J], BF16, "z")
+        HJ = J // 2
+        for h in range(2):
+            for t in range(4):
+                cols = slice(h * HJ, (h + 1) * HJ)
+                neg = tile([P, HJ], F32, "neg%d_%d" % (t, h))
+                nc.vector.tensor_tensor(
+                    out=neg[:], in0=dwin[t][:].indirect(half(p3, h)), in1=top[:, t, cols], op=ALU.subtract,
+                )
+                nc.scalar.activation(out=join[:, t, cols], in_=neg[:], func=ACT.Tanh, scale=-1.0)
+                if h == 0:
+                    nc.scalar.activation(
+                        out=z[:, t, cols], in_=join[:, t, cols], func=ACT.Copy, scale=gain_sb[:, t : t + 1]
+                    )
+
+        out_rows = out.rearrange("(p t) j -> p t j", t=4)
+        for h in range(2):
+            cols = slice(h * HJ, (h + 1) * HJ)
+            if h == 1:
+                for t in range(4):
+                    nc.vector.tensor_scalar(
+                        out=z[:, t, cols], in0=join[:, t, cols], scalar1=gain_sb[:, t : t + 1], scalar2=None,
+                        op0=ALU.mult,
+                    )
+            zi = tile([P, HJ, 4], BF16, "zi%d" % h)
+            nc.vector.tensor_copy(
+                zi[:].rearrange("p (c i) t -> p c t i", i=4),
+                z[:, :, cols].rearrange("p t (c i) -> p c t i", i=4),
+            )
+            zq = tile([P, HJ], U32, "zq%d" % h)
+            zs = tile([P, HJ], U8, "zs%d" % h)
+            nc.vector.quantize_mx(
+                out=zq[:].bitcast(FP8X4), scales=zs[:], in_=zi[:].rearrange("p j t -> p (j t)")
+            )
+            for u in range(2):
+                acc = bank(2 * h + u, "y%d%d" % (h, u))
+                for e in range(2):
+                    t = 2 * u + e
+                    nc.tensor.matmul_mx(
+                        out=acc[:, e * HJ : (e + 1) * HJ],
+                        lhsT=fp8_cols(w4d, t),
+                        lhsT_scale=w4sd[:, t * P : (t + 1) * P],
+                        rhs=zq[:].bitcast(FP8X4),
+                        rhs_scale=zs[:],
+                        start=True,
+                        stop=True,
+                    )
+                res = tile([P, 2, HJ], F32, "res%d%d" % (h, u))
+                nc.vector.tensor_tensor(
+                    out=res[:], in0=acc[:].rearrange("p (e j) -> p e j", e=2),
+                    in1=join[:, 2 * u : 2 * u + 2, cols], op=ALU.add,
+                )
+                nc.sync.dma_start(out=out_rows[:, 2 * u : 2 * u + 2, cols], in_=res[:])

@@ -47,12 +47,11 @@ def tile_list_haulage_permit_join_kernel(
             nc.vector.memset(plane[:].bitcast(I32), 0)
             return plane
 
-        def load_scales(queue, plane, scales):
-            passes = scales.shape[0]
+        def load_scales(plane, scales, first_row):
             for q in range(4):
-                queue.dma_start(
-                    out=plane[32 * q : 32 * q + 4 * passes, :].bitcast(I32),
-                    in_=scales[:, 4 * q : 4 * q + 4, :].bitcast(I32),
+                nc.sync.dma_start(
+                    out=plane[32 * q + first_row : 32 * q + first_row + 4, :].bitcast(I32),
+                    in_=scales[0, 4 * q : 4 * q + 4, :].bitcast(I32),
                 )
 
         def load_table(words, a, name, tag=None):
@@ -98,14 +97,17 @@ def tile_list_haulage_permit_join_kernel(
         def halves(picked):
             return [picked[:, h * N : (h + 1) * N] for h in range(2)]
 
-        def quantise_weight(raw, name, tag):
-            rounded = tile([P, 4 * H], BF16, name + "_bf", tag)
+        def round_weight(raw, name, tag):
+            rounded = tile([P, 4 * H], BF16, name, tag)
             nc.scalar.activation(
                 out=rounded[:].rearrange("p (t m j) -> p m t j", t=4, j=4),
                 in_=raw[:].rearrange("p j (m t) -> p m t j", t=4),
                 func=ACT.Copy,
             )
-            codes = tile([P, H], U32, name + "_codes")
+            return rounded
+
+        def quantise_weight(rounded, name, tag):
+            codes = tile([P, H], U32, name + "_codes", tag)
             plane = tile([P, H], U8, name + "_plane")
             nc.vector.quantize_mx(out=codes[:].bitcast(FP8X4), scales=plane[:], in_=rounded[:])
             return codes, plane
@@ -116,73 +118,8 @@ def tile_list_haulage_permit_join_kernel(
         def fp8_cols(codes, t):
             return codes[:, t * P : (t + 1) * P].bitcast(FP8X4)
 
-        s2 = zeroed_plane(T, "s2", "raw2")
-        w2s = zeroed_plane(H, "w2s")
-        l1 = load_list(offs, "l1")
-        s1 = load_scale_rows(tab_scales, "s1", "raw1")
-        l3 = load_list(offs3, "l3")
-        s3 = load_scale_rows(tab3_scales, "s3", "tabB")
-        g1s = zeroed_plane(S, "g1s")
-        g3s = zeroed_plane(S, "g3s")
-        w2raw = tile([P, 2 * H], U8, "w2raw")
-        nc.sync.dma_start(out=w2raw[:].bitcast(I32), in_=w2_words[0].bitcast(I32))
-        l2 = load_list(offs2, "l2")
-        t2 = tile([P, T], I32, "t2", "tabA")
-        nc.sync.dma_start(out=t2[:, 0:2048], in_=words_view(tab2_words, 0)[:, 0:2048])
-        p1 = load_list(pos1, "p1")
-        p2 = load_list(pos2, "p2")
-        p3 = load_list(pos3, "p3")
-        nc.sync.dma_start(out=t2[:, 2048:T], in_=words_view(tab2_words, 0)[:, 2048:T])
-        load_scales(nc.sync, s2, tab2_scales)
-        w1raw0 = load_weight(w1, 0, "w1raw0", "raw0")
-        load_scales(nc.sync, w2s, w2_scales)
-
-        r1s = gather_scales(s1, l1[:], "r1s")
-        r3s = gather_scales(s3, l3[:], "r3s")
-        w2d = tile([P, 2 * H], U8, "w2d")
-        nc.vector.tensor_copy(
-            w2d[:].rearrange("p (t q b) -> p t q b", t=4, b=2),
-            w2raw[:].rearrange("p (q t b) -> p t q b", t=4, b=2),
-        )
-        place_scale_rows(r1s, g1s, 0, 2)
-        w1raw1 = load_weight(w1, 1, "w1raw1", "raw1")
-        place_scale_rows(r1s, g1s, 2, 8)
-        t10 = load_table(tab_words, 0, "t10", "tabB")
-        place_scale_rows(r3s, g3s, 0, 6)
-        w2sd = tile([P, H], U8, "w2sd")
-        nc.vector.tensor_copy(
-            w2sd[:].rearrange("p (t q) -> p t q", t=4), w2s[:].rearrange("p (q t) -> p t q", t=4)
-        )
-        g2s, g2 = [], []
-        for h in range(2):
-            g2s.append(gather_scales(s2, half(l2, h), "g2s%d" % h))
-            g2.append(gather_words(t2, half(l2, h), "g2%d" % h))
-        w3raw0 = load_weight(w3, 0, "w3raw0", "raw2")
-        place_scale_rows(r3s, g3s, 6, 8)
-        t11 = load_table(tab_words, 1, "t11", "tabA")
-        w1q0 = quantise_weight(w1raw0, "w1q0", "bf0")
-
-        order = [(t, h) for h in range(2) for t in range(4)]
-        bwin = [tile([P, S], F32, "bwin%d" % t) for t in range(4)]
-        for t, h in order:
-                acc = bank(2 * t + h, "b%d%d" % (t, h))
-                nc.tensor.matmul_mx(
-                    out=acc[:],
-                    lhsT=w2d[:, 2 * t * P : 2 * (t + 1) * P].bitcast(FP4X4),
-                    lhsT_scale=w2sd[:, t * P : (t + 1) * P],
-                    rhs=g2[h][:].bitcast(FP8X4),
-                    rhs_scale=g2s[h][:],
-                    start=True,
-                    stop=True,
-                )
-                nc.scalar.copy(out=bwin[t][:, h * N : (h + 1) * N], in_=acc[:])
-
-        w1q = [w1q0, quantise_weight(w1raw1, "w1q1", "bf1")]
-        w3raw1 = load_weight(w3, 1, "w3raw1", "raw0")
-
-        top = tile([P, 4, J], F32, "top")
-        for t in range(4):
-            nc.vector.tensor_copy(top[:, t, :], bwin[t][:].indirect(p2[:]))
+        def deal(dealt, raw):
+            nc.vector.tensor_copy(dealt.rearrange("p (t q) -> p t q", t=4), raw.rearrange("p (q t) -> p t q", t=4))
 
         def mx_pass(accs, order, wq, picked, picked_scales, a):
             codes, plane = wq
@@ -198,89 +135,139 @@ def tile_list_haulage_permit_join_kernel(
                 )
 
         by_slice = [(t, h) for t in range(4) for h in range(2)]
+        by_pair = [(2 * u + e, h) for u in range(2) for h in range(2) for e in range(2)]
+
+        l1 = load_list(offs, "l1")
+        s2 = zeroed_plane(T, "s2", "tabC")
+        s1 = load_scale_rows(tab_scales, "s1", "tabB")
+        w2s = zeroed_plane(H, "w2s")
+        t2 = tile([P, T], I32, "t2", "tabA")
+        nc.sync.dma_start(out=t2[:, 0:2048], in_=words_view(tab2_words, 0)[:, 0:2048])
+        l2 = load_list(offs2, "l2")
+        load_scales(s2, tab2_scales, 0)
+        w2raw = tile([P, 2 * H], U8, "w2raw")
+        nc.sync.dma_start(out=w2raw[:].bitcast(I32), in_=w2_words[0].bitcast(I32))
+        nc.sync.dma_start(out=t2[:, 2048:T], in_=words_view(tab2_words, 0)[:, 2048:T])
+        load_scales(w2s, w4_scales, 4)
+        w1raw0 = load_weight(w1, 0, "w1raw0", "raw0")
+        load_scales(w2s, w2_scales, 0)
+        l3 = load_list(offs3, "l3")
+        s3 = load_scale_rows(tab3_scales, "s3", "s3")
+        w1raw1 = load_weight(w1, 1, "w1raw1", "raw1")
+        p2 = load_list(pos2, "p2")
+        g1s = zeroed_plane(S, "g1s")
+        g3s = zeroed_plane(S, "g3s")
+
+        r1s = gather_scales(s1, l1[:], "r1s")
+        place_scale_rows(r1s, g1s, 0, 2)
+        t10 = load_table(tab_words, 0, "t10", "tabB")
+        g2s = halves(gather_scales(s2, l2[:], "g2s"))
+        w2d = tile([P, 2 * H], U8, "w2d")
+        deal(w2d[:].bitcast(U16), w2raw[:].bitcast(U16))
+        g2 = halves(gather_words(t2, l2[:], "g2"))
+        w2sd = tile([P, H], U8, "w2sd")
+        deal(w2sd[:], w2s[:])
+        r3s = gather_scales(s3, l3[:], "r3s")
+        place_scale_rows(r1s, g1s, 2, 8)
+        t11 = load_table(tab_words, 1, "t11", "tabC")
+        place_scale_rows(r3s, g3s, 0, 4)
+        w1q = [quantise_weight(round_weight(w1raw0, "w1bf0", "bf0"), "w1q0", "s3")]
+        w3raw0 = load_weight(w3, 0, "w3raw0", "raw0")
+        place_scale_rows(r3s, g3s, 4, 8)
+        p1 = load_list(pos1, "p1")
+        t30 = load_table(tab3_words, 0, "t30", "tabA")
+
+        bwin = [tile([P, S], F32, "bwin%d" % t) for t in range(4)]
+        for t, h in by_slice:
+            acc = bank(2 * t + h, "b%d%d" % (t, h))
+            nc.tensor.matmul_mx(
+                out=acc[:],
+                lhsT=w2d[:, 2 * t * P : 2 * (t + 1) * P].bitcast(FP4X4),
+                lhsT_scale=w2sd[:, t * P : (t + 1) * P],
+                rhs=g2[h].bitcast(FP8X4),
+                rhs_scale=g2s[h],
+                start=True,
+                stop=True,
+            )
+            nc.scalar.copy(out=bwin[t][:, h * N : (h + 1) * N], in_=acc[:])
+        w1bf1 = round_weight(w1raw1, "w1bf1", "bf1")
+        w3raw1 = load_weight(w3, 1, "w3raw1", "raw1")
+
+        top = [tile([P, J], F32, "top%d" % t) for t in range(3)]
+        for t in range(3):
+            nc.vector.tensor_copy(top[t][:], bwin[t][:].indirect(p2[:]))
+
         g10 = halves(gather_words(t10, l1[:], "g10"))
-        t30 = load_table(tab3_words, 0, "t30", "tabB")
-        w3q0 = quantise_weight(w3raw0, "w3q0", "bf0")
-        w4raw = tile([P, H], I32, "w4raw", "g21")
-        nc.sync.dma_start(out=w4raw[:], in_=words_view(w4_words, 0))
-        load_scales(nc.sync, w2s, w4_scales)
+        w1q.append(quantise_weight(w1bf1, "w1q1", "tabB"))
         g11 = [gather_words(t11, half(l1, h), "g11%d" % h)[:] for h in range(2)]
-        t31 = load_table(tab3_words, 1, "t31", "tabA")
+        top.append(tile([P, J], F32, "top3", "tabC"))
+        nc.vector.tensor_copy(top[3][:], bwin[3][:].indirect(p2[:]))
         accs = {(t, h): bank(2 * t + h, "a%d%d" % (t, h)) for t, h in by_slice}
         mx_pass(accs, by_slice, w1q[0], g10, g1s, 0)
-        mx_pass(accs, order, w1q[1], g11, g1s, 1)
+        mx_pass(accs, by_pair, w1q[1], g11, g1s, 1)
+        t31 = load_table(tab3_words, 1, "t31", "tabB")
+        w4raw = tile([P, H], I32, "w4raw")
+        nc.sync.dma_start(out=w4raw[:], in_=words_view(w4_words, 0))
+        p3 = load_list(pos3, "p3")
+        gain_sb = tile([P, 4], F32, "gain_sb")
+        nc.sync.dma_start(out=gain_sb[:], in_=gain.rearrange("(p t) -> p t", t=4))
         awin = [tile([P, S], F32, "awin%d" % t) for t in range(4)]
-        for t, h in order:
+        for t, h in by_pair:
             nc.scalar.copy(out=awin[t][:, h * N : (h + 1) * N], in_=accs[t, h][:])
 
-        w4d = tile([P, H], I32, "w4d", "g110")
-        nc.vector.tensor_copy(
-            w4d[:].rearrange("p (t q) -> p t q", t=4), w4raw[:].rearrange("p (q t) -> p t q", t=4)
-        )
-        w4sd = tile([P, H], U8, "w4sd", "g111")
-        nc.vector.tensor_copy(
-            w4sd[:].rearrange("p (t q) -> p t q", t=4), w2s[:].rearrange("p (q t) -> p t q", t=4)
-        )
+        w4d = tile([P, H], I32, "w4d")
+        deal(w4d[:], w4raw[:])
 
-        w3q = [w3q0, quantise_weight(w3raw1, "w3q1", "bf1")]
-        gain_sb = tile([P, 4], F32, "gain_sb", "g10")
-        nc.sync.dma_start(out=gain_sb[:], in_=gain.rearrange("(p t) -> p t", t=4))
-        ga = tile([P, 4, J], F32, "ga")
-        for u in range(2):
-            for t in (2 * u, 2 * u + 1):
-                nc.vector.tensor_copy(ga[:, t, :], awin[t][:].indirect(p1[:]))
-            nc.vector.tensor_tensor(
-                out=top[:, 2 * u : 2 * u + 2, :], in0=ga[:, 2 * u : 2 * u + 2, :],
-                in1=top[:, 2 * u : 2 * u + 2, :], op=ALU.max,
-            )
+        def larger_demand(t, tag):
+            ga = tile([P, J], F32, "ga%d" % t, tag)
+            nc.vector.tensor_copy(ga[:], awin[t][:].indirect(p1[:]))
+            nc.vector.tensor_tensor(out=top[t][:], in0=ga[:], in1=top[t][:], op=ALU.max)
+
+        for t in range(3):
+            larger_demand(t, None)
 
         g30 = halves(gather_words(t30, l3[:], "g30"))
+        w3q = [quantise_weight(round_weight(w3raw0, "w3bf0", "bf0"), "w3q0", "tabA")]
+        w3bf1 = round_weight(w3raw1, "w3bf1", "bf1")
         accs = {(t, h): bank(2 * t + h, "d%d%d" % (t, h)) for t, h in by_slice}
         mx_pass(accs, by_slice, w3q[0], g30, g3s, 0)
-        g31 = [gather_words(t31, half(l3, h), "g31%d" % h)[:] for h in range(2)]
-        mx_pass(accs, order, w3q[1], g31, g3s, 1)
+        g31 = halves(gather_words(t31, l3[:], "g31"))
+        w3q.append(quantise_weight(w3bf1, "w3q1", "tabB"))
+        larger_demand(3, "bf1")
+        mx_pass(accs, by_slice, w3q[1], g31, g3s, 1)
         dwin = [tile([P, S], F32, "dwin%d" % t, "bwin%d" % t) for t in range(4)]
-        for t, h in order:
-            if (t, h) in ((2, 0), (3, 0)):
-                nc.vector.tensor_copy(dwin[t][:, h * N : (h + 1) * N], accs[t, h][:])
-            else:
-                nc.scalar.copy(out=dwin[t][:, h * N : (h + 1) * N], in_=accs[t, h][:])
+        for t, h in by_slice:
+            nc.scalar.copy(out=dwin[t][:, h * N : (h + 1) * N], in_=accs[t, h][:])
 
         join = tile([P, 4, J], F32, "join")
         z = tile([P, 4, J], BF16, "z")
         HJ = J // 2
-        for h in range(2):
-            for t in range(4):
-                cols = slice(h * HJ, (h + 1) * HJ)
-                neg = tile([P, HJ], F32, "neg%d_%d" % (t, h))
-                nc.vector.tensor_tensor(
-                    out=neg[:], in0=dwin[t][:].indirect(half(p3, h)), in1=top[:, t, cols], op=ALU.subtract,
-                )
-                nc.scalar.activation(out=join[:, t, cols], in_=neg[:], func=ACT.Tanh, scale=-1.0)
-                if h == 0:
-                    nc.scalar.activation(
-                        out=z[:, t, cols], in_=join[:, t, cols], func=ACT.Copy, scale=gain_sb[:, t : t + 1]
-                    )
+        for t in range(4):
+            neg = tile([P, J], F32, "neg%d" % t)
+            nc.vector.tensor_tensor(out=neg[:], in0=dwin[t][:].indirect(p3[:]), in1=top[t][:], op=ALU.subtract)
+            nc.scalar.activation(out=join[:, t, :], in_=neg[:], func=ACT.Tanh, scale=-1.0)
+        for t in range(4):
+            nc.vector.tensor_scalar(
+                out=z[:, t, :], in0=join[:, t, :], scalar1=gain_sb[:, t : t + 1], scalar2=None, op0=ALU.mult
+            )
 
         out_rows = out.rearrange("(p t) j -> p t j", t=4)
+        quantised = []
         for h in range(2):
-            cols = slice(h * HJ, (h + 1) * HJ)
-            if h == 1:
-                for t in range(4):
-                    nc.vector.tensor_scalar(
-                        out=z[:, t, cols], in0=join[:, t, cols], scalar1=gain_sb[:, t : t + 1], scalar2=None,
-                        op0=ALU.mult,
-                    )
-            zi = tile([P, HJ, 4], BF16, "zi%d" % h)
+            zi = tile([P, HJ, 4], BF16, "zi%d" % h, "zi")
             nc.vector.tensor_copy(
                 zi[:].rearrange("p (c i) t -> p c t i", i=4),
-                z[:, :, cols].rearrange("p t (c i) -> p c t i", i=4),
+                z[:, :, h * HJ : (h + 1) * HJ].rearrange("p t (c i) -> p c t i", i=4),
             )
             zq = tile([P, HJ], U32, "zq%d" % h)
             zs = tile([P, HJ], U8, "zs%d" % h)
             nc.vector.quantize_mx(
                 out=zq[:].bitcast(FP8X4), scales=zs[:], in_=zi[:].rearrange("p j t -> p (j t)")
             )
+            quantised.append((zq, zs))
+        for h in range(2):
+            cols = slice(h * HJ, (h + 1) * HJ)
+            zq, zs = quantised[h]
             for u in range(2):
                 acc = bank(2 * h + u, "y%d%d" % (h, u))
                 for e in range(2):
@@ -288,13 +275,13 @@ def tile_list_haulage_permit_join_kernel(
                     nc.tensor.matmul_mx(
                         out=acc[:, e * HJ : (e + 1) * HJ],
                         lhsT=fp8_cols(w4d, t),
-                        lhsT_scale=w4sd[:, t * P : (t + 1) * P],
+                        lhsT_scale=w2sd[4:P, t * P : (t + 1) * P],
                         rhs=zq[:].bitcast(FP8X4),
                         rhs_scale=zs[:],
                         start=True,
                         stop=True,
                     )
-                res = tile([P, 2, HJ], F32, "res%d%d" % (h, u))
+                res = tile([P, 2, HJ], F32, "res%d%d" % (h, u), "zi" if (h, u) == (0, 0) else None)
                 nc.vector.tensor_tensor(
                     out=res[:], in0=acc[:].rearrange("p (e j) -> p e j", e=2),
                     in1=join[:, 2 * u : 2 * u + 2, cols], op=ALU.add,

@@ -47,9 +47,9 @@ def tile_list_haulage_permit_join_kernel(
             nc.vector.memset(plane[:].bitcast(I32), 0)
             return plane
 
-        def load_scales(plane, scales, first_row):
+        def load_scales(queue, plane, scales, first_row):
             for q in range(4):
-                nc.sync.dma_start(
+                queue.dma_start(
                     out=plane[32 * q + first_row : 32 * q + first_row + 4, :].bitcast(I32),
                     in_=scales[0, 4 * q : 4 * q + 4, :].bitcast(I32),
                 )
@@ -77,13 +77,14 @@ def tile_list_haulage_permit_join_kernel(
             nc.vector.tensor_copy(picked[:], rows[:].indirect(lst))
             return picked
 
-        def place_scale_rows(picked, plane, first_move, last_move):
-            for a, q in [divmod(i, 4) for i in range(first_move, last_move)]:
-                first = 96 + 16 * a + 4 * q
-                nc.sync.dma_start(
-                    out=plane[32 * q + 4 * a : 32 * q + 4 * a + 4, :].bitcast(I32),
-                    in_=picked[first : first + 4, :].bitcast(I32),
-                )
+        def place_scale_rows(picked, plane):
+            for a in range(2):
+                for q in range(4):
+                    first = 96 + 16 * a + 4 * q
+                    nc.gpsimd.dma_start(
+                        out=plane[32 * q + 4 * a : 32 * q + 4 * a + 4, :].bitcast(I32),
+                        in_=picked[first : first + 4, :].bitcast(I32),
+                    )
 
         def gather_words(table, lst, name):
             picked = tile([P, lst.shape[1] * 16], U32, name)
@@ -144,13 +145,13 @@ def tile_list_haulage_permit_join_kernel(
         t2 = tile([P, T], I32, "t2", "tabA")
         nc.sync.dma_start(out=t2[:, 0:2048], in_=words_view(tab2_words, 0)[:, 0:2048])
         l2 = load_list(offs2, "l2")
-        load_scales(s2, tab2_scales, 0)
+        load_scales(nc.sync, s2, tab2_scales, 0)
         w2raw = tile([P, 2 * H], U8, "w2raw")
         nc.sync.dma_start(out=w2raw[:].bitcast(I32), in_=w2_words[0].bitcast(I32))
         nc.sync.dma_start(out=t2[:, 2048:T], in_=words_view(tab2_words, 0)[:, 2048:T])
-        load_scales(w2s, w4_scales, 4)
+        load_scales(nc.gpsimd, w2s, w4_scales, 4)
         w1raw0 = load_weight(w1, 0, "w1raw0", "raw0")
-        load_scales(w2s, w2_scales, 0)
+        load_scales(nc.sync, w2s, w2_scales, 0)
         l3 = load_list(offs3, "l3")
         s3 = load_scale_rows(tab3_scales, "s3", "s3")
         w1raw1 = load_weight(w1, 1, "w1raw1", "raw1")
@@ -159,7 +160,7 @@ def tile_list_haulage_permit_join_kernel(
         g3s = zeroed_plane(S, "g3s")
 
         r1s = gather_scales(s1, l1[:], "r1s")
-        place_scale_rows(r1s, g1s, 0, 2)
+        place_scale_rows(r1s, g1s)
         t10 = load_table(tab_words, 0, "t10", "tabB")
         g2s = halves(gather_scales(s2, l2[:], "g2s"))
         w2d = tile([P, 2 * H], U8, "w2d")
@@ -168,12 +169,10 @@ def tile_list_haulage_permit_join_kernel(
         w2sd = tile([P, H], U8, "w2sd")
         deal(w2sd[:], w2s[:])
         r3s = gather_scales(s3, l3[:], "r3s")
-        place_scale_rows(r1s, g1s, 2, 8)
         t11 = load_table(tab_words, 1, "t11", "tabC")
-        place_scale_rows(r3s, g3s, 0, 4)
+        place_scale_rows(r3s, g3s)
         w1q = [quantise_weight(round_weight(w1raw0, "w1bf0", "bf0"), "w1q0", "s3")]
         w3raw0 = load_weight(w3, 0, "w3raw0", "raw0")
-        place_scale_rows(r3s, g3s, 4, 8)
         p1 = load_list(pos1, "p1")
         t30 = load_table(tab3_words, 0, "t30", "tabA")
 
@@ -223,37 +222,46 @@ def tile_list_haulage_permit_join_kernel(
             nc.vector.tensor_copy(ga[:], awin[t][:].indirect(p1[:]))
             nc.vector.tensor_tensor(out=top[t][:], in0=ga[:], in1=top[t][:], op=ALU.max)
 
-        for t in range(3):
+        for t in range(2):
             larger_demand(t, None)
 
         g30 = halves(gather_words(t30, l3[:], "g30"))
         w3q = [quantise_weight(round_weight(w3raw0, "w3bf0", "bf0"), "w3q0", "tabA")]
+        larger_demand(2, "bf0")
         w3bf1 = round_weight(w3raw1, "w3bf1", "bf1")
         accs = {(t, h): bank(2 * t + h, "d%d%d" % (t, h)) for t, h in by_slice}
         mx_pass(accs, by_slice, w3q[0], g30, g3s, 0)
-        g31 = halves(gather_words(t31, l3[:], "g31"))
-        w3q.append(quantise_weight(w3bf1, "w3q1", "tabB"))
-        larger_demand(3, "bf1")
-        mx_pass(accs, by_slice, w3q[1], g31, g3s, 1)
+        w3q.append(quantise_weight(w3bf1, "w3q1", None))
+        g31 = [gather_words(t31, half(l3, h), "g31%d" % h)[:] for h in range(2)]
+        larger_demand(3, "tabB")
+        mx_pass(accs, by_pair, w3q[1], g31, g3s, 1)
         dwin = [tile([P, S], F32, "dwin%d" % t, "bwin%d" % t) for t in range(4)]
-        for t, h in by_slice:
+        for t, h in by_pair:
             nc.scalar.copy(out=dwin[t][:, h * N : (h + 1) * N], in_=accs[t, h][:])
 
         join = tile([P, 4, J], F32, "join")
         z = tile([P, 4, J], BF16, "z")
         HJ = J // 2
-        for t in range(4):
-            neg = tile([P, J], F32, "neg%d" % t)
-            nc.vector.tensor_tensor(out=neg[:], in0=dwin[t][:].indirect(p3[:]), in1=top[t][:], op=ALU.subtract)
-            nc.scalar.activation(out=join[:, t, :], in_=neg[:], func=ACT.Tanh, scale=-1.0)
-        for t in range(4):
-            nc.vector.tensor_scalar(
-                out=z[:, t, :], in0=join[:, t, :], scalar1=gain_sb[:, t : t + 1], scalar2=None, op0=ALU.mult
+        for t, j0, j1 in [(0, 0, J), (1, 0, J), (2, 0, J), (3, 0, HJ), (3, HJ, J)]:
+            neg = tile([P, j1 - j0], F32, "neg%d_%d" % (t, j0))
+            nc.vector.tensor_tensor(
+                out=neg[:], in0=dwin[t][:].indirect(p3[:, j0 // 16 : j1 // 16]), in1=top[t][:, j0:j1],
+                op=ALU.subtract,
             )
+            nc.scalar.activation(out=join[:, t, j0:j1], in_=neg[:], func=ACT.Tanh, scale=-1.0)
+            if t == 0:
+                nc.scalar.activation(
+                    out=z[:, t, j0:j1], in_=join[:, t, j0:j1], func=ACT.Copy, scale=gain_sb[:, t : t + 1]
+                )
 
         out_rows = out.rearrange("(p t) j -> p t j", t=4)
         quantised = []
         for h in range(2):
+            for t in range(1, 4):
+                cols = slice(h * HJ, (h + 1) * HJ)
+                nc.vector.tensor_scalar(
+                    out=z[:, t, cols], in0=join[:, t, cols], scalar1=gain_sb[:, t : t + 1], scalar2=None, op0=ALU.mult
+                )
             zi = tile([P, HJ, 4], BF16, "zi%d" % h, "zi")
             nc.vector.tensor_copy(
                 zi[:].rearrange("p (c i) t -> p c t i", i=4),

@@ -47,10 +47,10 @@ def tile_list_haulage_permit_join_kernel(
             nc.vector.memset(plane[:].bitcast(I32), 0)
             return plane
 
-        def load_scales(queue, plane, scales, first_row):
+        def load_scales(plane, scales):
             for q in range(4):
-                queue.dma_start(
-                    out=plane[32 * q + first_row : 32 * q + first_row + 4, :].bitcast(I32),
+                nc.sync.dma_start(
+                    out=plane[32 * q : 32 * q + 4, :].bitcast(I32),
                     in_=scales[0, 4 * q : 4 * q + 4, :].bitcast(I32),
                 )
 
@@ -77,14 +77,12 @@ def tile_list_haulage_permit_join_kernel(
             nc.vector.tensor_copy(picked[:], rows[:].indirect(lst))
             return picked
 
-        def place_scale_rows(picked, plane):
-            for a in range(2):
-                for q in range(4):
-                    first = 96 + 16 * a + 4 * q
-                    nc.gpsimd.dma_start(
-                        out=plane[32 * q + 4 * a : 32 * q + 4 * a + 4, :].bitcast(I32),
-                        in_=picked[first : first + 4, :].bitcast(I32),
-                    )
+        def place_scale_rows(picked, plane, a):
+            for q in range(4):
+                first = 96 + 16 * a + 4 * q
+                nc.sync.dma_start(
+                    out=plane[32 * q : 32 * q + 4, :].bitcast(I32), in_=picked[first : first + 4, :].bitcast(I32)
+                )
 
         def gather_words(table, lst, name):
             picked = tile([P, lst.shape[1] * 16], U32, name)
@@ -130,7 +128,7 @@ def tile_list_haulage_permit_join_kernel(
                     lhsT=fp8_cols(codes, t),
                     lhsT_scale=plane[:, t * P : (t + 1) * P],
                     rhs=picked[h].bitcast(FP8X4),
-                    rhs_scale=picked_scales[4 * a : P, h * N : (h + 1) * N],
+                    rhs_scale=picked_scales[a][:, h * N : (h + 1) * N],
                     start=(a == 0),
                     stop=(a == 1),
                 )
@@ -145,22 +143,23 @@ def tile_list_haulage_permit_join_kernel(
         t2 = tile([P, T], I32, "t2", "tabA")
         nc.sync.dma_start(out=t2[:, 0:2048], in_=words_view(tab2_words, 0)[:, 0:2048])
         l2 = load_list(offs2, "l2")
-        load_scales(nc.sync, s2, tab2_scales, 0)
+        load_scales(s2, tab2_scales)
         w2raw = tile([P, 2 * H], U8, "w2raw")
         nc.sync.dma_start(out=w2raw[:].bitcast(I32), in_=w2_words[0].bitcast(I32))
         nc.sync.dma_start(out=t2[:, 2048:T], in_=words_view(tab2_words, 0)[:, 2048:T])
-        load_scales(nc.gpsimd, w2s, w4_scales, 4)
         w1raw0 = load_weight(w1, 0, "w1raw0", "raw0")
-        load_scales(nc.sync, w2s, w2_scales, 0)
+        load_scales(w2s, w2_scales)
         l3 = load_list(offs3, "l3")
         s3 = load_scale_rows(tab3_scales, "s3", "s3")
         w1raw1 = load_weight(w1, 1, "w1raw1", "raw1")
         p2 = load_list(pos2, "p2")
-        g1s = zeroed_plane(S, "g1s")
-        g3s = zeroed_plane(S, "g3s")
+        planes = [zeroed_plane(2 * S, "planes%d" % a) for a in range(2)]
+        g1s = [plane[:, 0:S] for plane in planes]
+        g3s = [plane[:, S : 2 * S] for plane in planes]
+        w4s = zeroed_plane(H, "w4s")
+        rows = tile([P, 2 * S], U8, "rows")
 
-        r1s = gather_scales(s1, l1[:], "r1s")
-        place_scale_rows(r1s, g1s)
+        nc.vector.tensor_copy(rows[:, 0:S], s1[:].indirect(l1[:]))
         t10 = load_table(tab_words, 0, "t10", "tabB")
         g2s = halves(gather_scales(s2, l2[:], "g2s"))
         w2d = tile([P, 2 * H], U8, "w2d")
@@ -168,9 +167,10 @@ def tile_list_haulage_permit_join_kernel(
         g2 = halves(gather_words(t2, l2[:], "g2"))
         w2sd = tile([P, H], U8, "w2sd")
         deal(w2sd[:], w2s[:])
-        r3s = gather_scales(s3, l3[:], "r3s")
+        nc.vector.tensor_copy(rows[:, S : 2 * S], s3[:].indirect(l3[:]))
+        place_scale_rows(rows, planes[0], 0)
         t11 = load_table(tab_words, 1, "t11", "tabC")
-        place_scale_rows(r3s, g3s)
+        place_scale_rows(rows, planes[1], 1)
         w1q = [quantise_weight(round_weight(w1raw0, "w1bf0", "bf0"), "w1q0", "s3")]
         w3raw0 = load_weight(w3, 0, "w3raw0", "raw0")
         p1 = load_list(pos1, "p1")
@@ -205,6 +205,7 @@ def tile_list_haulage_permit_join_kernel(
         mx_pass(accs, by_slice, w1q[0], g10, g1s, 0)
         mx_pass(accs, by_pair, w1q[1], g11, g1s, 1)
         t31 = load_table(tab3_words, 1, "t31", "tabB")
+        load_scales(w4s, w4_scales)
         w4raw = tile([P, H], I32, "w4raw")
         nc.sync.dma_start(out=w4raw[:], in_=words_view(w4_words, 0))
         p3 = load_list(pos3, "p3")
@@ -216,24 +217,32 @@ def tile_list_haulage_permit_join_kernel(
 
         w4d = tile([P, H], I32, "w4d")
         deal(w4d[:], w4raw[:])
+        w4sd = tile([P, H], U8, "w4sd")
+        deal(w4sd[:], w4s[:])
 
-        def larger_demand(t, tag):
+        def pick_a(t, tag):
             ga = tile([P, J], F32, "ga%d" % t, tag)
             nc.vector.tensor_copy(ga[:], awin[t][:].indirect(p1[:]))
-            nc.vector.tensor_tensor(out=top[t][:], in0=ga[:], in1=top[t][:], op=ALU.max)
+            return ga
 
-        for t in range(2):
-            larger_demand(t, None)
+        def larger_demand(t, ga, tag):
+            larger = tile([P, J], F32, "larger%d" % t, tag)
+            nc.vector.tensor_tensor(out=larger[:], in0=ga[:], in1=top[t][:], op=ALU.max)
+            top[t] = larger
 
+        ga = [pick_a(t, None) for t in range(3)]
+        for t in range(3):
+            larger_demand(t, ga[t], None)
+
+        w3q = [quantise_weight(round_weight(w3raw0, "w3bf0", "bf0"), "w3q0", None)]
         g30 = halves(gather_words(t30, l3[:], "g30"))
-        w3q = [quantise_weight(round_weight(w3raw0, "w3bf0", "bf0"), "w3q0", "tabA")]
-        larger_demand(2, "bf0")
+        ga3 = pick_a(3, "tabA")
         w3bf1 = round_weight(w3raw1, "w3bf1", "bf1")
         accs = {(t, h): bank(2 * t + h, "d%d%d" % (t, h)) for t, h in by_slice}
         mx_pass(accs, by_slice, w3q[0], g30, g3s, 0)
         w3q.append(quantise_weight(w3bf1, "w3q1", None))
         g31 = [gather_words(t31, half(l3, h), "g31%d" % h)[:] for h in range(2)]
-        larger_demand(3, "tabB")
+        larger_demand(3, ga3, "tabB")
         mx_pass(accs, by_pair, w3q[1], g31, g3s, 1)
         dwin = [tile([P, S], F32, "dwin%d" % t, "bwin%d" % t) for t in range(4)]
         for t, h in by_pair:
@@ -262,8 +271,9 @@ def tile_list_haulage_permit_join_kernel(
                 nc.vector.tensor_scalar(
                     out=z[:, t, cols], in0=join[:, t, cols], scalar1=gain_sb[:, t : t + 1], scalar2=None, op0=ALU.mult
                 )
-            zi = tile([P, HJ, 4], BF16, "zi%d" % h, "zi")
-            nc.vector.tensor_copy(
+            zi = tile([P, HJ, 4], BF16, "zi%d" % h)
+            weave = nc.vector.tensor_copy if h == 0 else nc.scalar.copy
+            weave(
                 zi[:].rearrange("p (c i) t -> p c t i", i=4),
                 z[:, :, h * HJ : (h + 1) * HJ].rearrange("p t (c i) -> p c t i", i=4),
             )
@@ -277,21 +287,18 @@ def tile_list_haulage_permit_join_kernel(
             cols = slice(h * HJ, (h + 1) * HJ)
             zq, zs = quantised[h]
             for u in range(2):
-                acc = bank(2 * h + u, "y%d%d" % (h, u))
+                res = tile([P, 2, HJ], F32, "res%d%d" % (h, u))
                 for e in range(2):
                     t = 2 * u + e
+                    acc = bank(4 * h + t, "y%d%d" % (h, t))
                     nc.tensor.matmul_mx(
-                        out=acc[:, e * HJ : (e + 1) * HJ],
+                        out=acc[:, 0:HJ],
                         lhsT=fp8_cols(w4d, t),
-                        lhsT_scale=w2sd[4:P, t * P : (t + 1) * P],
+                        lhsT_scale=w4sd[:, t * P : (t + 1) * P],
                         rhs=zq[:].bitcast(FP8X4),
                         rhs_scale=zs[:],
                         start=True,
                         stop=True,
                     )
-                res = tile([P, 2, HJ], F32, "res%d%d" % (h, u), "zi" if (h, u) == (0, 0) else None)
-                nc.vector.tensor_tensor(
-                    out=res[:], in0=acc[:].rearrange("p (e j) -> p e j", e=2),
-                    in1=join[:, 2 * u : 2 * u + 2, cols], op=ALU.add,
-                )
+                    nc.vector.tensor_tensor(out=res[:, e, :], in0=acc[:, 0:HJ], in1=join[:, t, cols], op=ALU.add)
                 nc.sync.dma_start(out=out_rows[:, 2 * u : 2 * u + 2, cols], in_=res[:])

from contextlib import ExitStack

import concourse.mybir as mybir

F32 = mybir.dt.float32
BF16 = mybir.dt.bfloat16
I32 = mybir.dt.int32
U32 = mybir.dt.uint32
U16 = mybir.dt.uint16
U8 = mybir.dt.uint8
FP8X4 = mybir.dt.float8_e4m3fn_x4
FP4X4 = mybir.dt.float4_e2m1fn_x4
ACT = mybir.ActivationFunctionType
ALU = mybir.AluOpType

P = 128
T = 4096
S = 1024
J = 512
H = 512
N = 512
FLOPS = 2952790016


def tile_list_haulage_permit_join_kernel(
    tc, tab_words, tab_scales, tab2_words, tab2_scales, tab3_words, tab3_scales, offs, offs2, offs3,
    pos1, pos2, pos3, w1, w2_words, w2_scales, w3, gain, w4_words, w4_scales, out,
):
    nc = tc.nc
    with ExitStack() as ctx:
        keep = ctx.enter_context(tc.tile_pool(name="keep", bufs=1))
        psum = ctx.enter_context(tc.psum_pool(name="psum", bufs=1))

        def tile(shape, dtype, name, tag=None):
            return keep.tile(shape, dtype, name=name, tag=tag or name, align_bytes=64)

        def load_list(src, name):
            lst = keep.tile(list(src.shape), U16, name=name)
            nc.sync.dma_start(lst[:], src)
            return lst

        def words_view(words, a):
            return words[a].rearrange("p n t -> p (n t)").bitcast(I32)

        def zeroed_plane(width, name, tag=None):
            plane = tile([P, width], U8, name, tag)
            nc.vector.memset(plane[:].bitcast(I32), 0)
            return plane

        def load_scales(plane, scales):
            for q in range(4):
                nc.sync.dma_start(
                    out=plane[32 * q : 32 * q + 4, :].bitcast(I32),
                    in_=scales[0, 4 * q : 4 * q + 4, :].bitcast(I32),
                )

        def load_table(words, a, name, tag=None):
            table = tile([P, T], I32, name, tag)
            nc.sync.dma_start(out=table[:], in_=words_view(words, a))
            return table

        def load_weight(w, a, name, tag):
            raw = tile([P, 4, H], F32, name, tag)
            nc.sync.dma_start(out=raw[:], in_=w[512 * a : 512 * (a + 1), :].rearrange("(p j) c -> p j c", j=4))
            return raw

        def load_scale_rows(scales, name, tag):
            rows = tile([P, T], U8, name, tag)
            nc.vector.memset(rows[0:96, :].bitcast(I32), 0)
            nc.sync.dma_start(
                out=rows[96:P, :].bitcast(I32), in_=scales.rearrange("a q n -> (a q) n").bitcast(I32)
            )
            return rows

        def gather_scales(rows, lst, name):
            picked = tile([P, lst.shape[1] * 16], U8, name)
            nc.vector.tensor_copy(picked[:], rows[:].indirect(lst))
            return picked

        def place_scale_rows(picked, plane, a):
            for q in range(4):
                first = 96 + 16 * a + 4 * q
                nc.sync.dma_start(
                    out=plane[32 * q : 32 * q + 4, :].bitcast(I32), in_=picked[first : first + 4, :].bitcast(I32)
                )

        def gather_words(table, lst, name):
            picked = tile([P, lst.shape[1] * 16], U32, name)
            nc.vector.tensor_copy(picked[:], table[:].bitcast(U32).indirect(lst))
            return picked

        def half(lst, h):
            columns = lst.shape[1] // 2
            return lst[:, h * columns : (h + 1) * columns]

        def halves(picked):
            return [picked[:, h * N : (h + 1) * N] for h in range(2)]

        def round_weight(raw, name, tag):
            rounded = tile([P, 4 * H], BF16, name, tag)
            nc.scalar.activation(
                out=rounded[:].rearrange("p (t m j) -> p m t j", t=4, j=4),
                in_=raw[:].rearrange("p j (m t) -> p m t j", t=4),
                func=ACT.Copy,
            )
            return rounded

        def quantise_weight(rounded, name, tag):
            codes = tile([P, H], U32, name + "_codes", tag)
            plane = tile([P, H], U8, name + "_plane")
            nc.vector.quantize_mx(out=codes[:].bitcast(FP8X4), scales=plane[:], in_=rounded[:])
            return codes, plane

        def bank(i, name):
            return psum.tile([P, N], F32, name=name, tag="bank%d" % i)

        def fp8_cols(codes, t):
            return codes[:, t * P : (t + 1) * P].bitcast(FP8X4)

        def deal(dealt, raw):
            nc.vector.tensor_copy(dealt.rearrange("p (t q) -> p t q", t=4), raw.rearrange("p (q t) -> p t q", t=4))

        def mx_pass(accs, order, wq, picked, picked_scales, a):
            codes, plane = wq
            for t, h in order:
                nc.tensor.matmul_mx(
                    out=accs[t, h][:],
                    lhsT=fp8_cols(codes, t),
                    lhsT_scale=plane[:, t * P : (t + 1) * P],
                    rhs=picked[h].bitcast(FP8X4),
                    rhs_scale=picked_scales[a][:, h * N : (h + 1) * N],
                    start=(a == 0),
                    stop=(a == 1),
                )

        by_slice = [(t, h) for t in range(4) for h in range(2)]
        by_pair = [(2 * u + e, h) for u in range(2) for h in range(2) for e in range(2)]

        l1 = load_list(offs, "l1")
        s2 = zeroed_plane(T, "s2", "tabC")
        s1 = load_scale_rows(tab_scales, "s1", "tabB")
        w2s = zeroed_plane(H, "w2s")
        t2 = tile([P, T], I32, "t2", "tabA")
        nc.sync.dma_start(out=t2[:, 0:2048], in_=words_view(tab2_words, 0)[:, 0:2048])
        l2 = load_list(offs2, "l2")
        load_scales(s2, tab2_scales)
        w2raw = tile([P, 2 * H], U8, "w2raw")
        nc.sync.dma_start(out=w2raw[:].bitcast(I32), in_=w2_words[0].bitcast(I32))
        nc.sync.dma_start(out=t2[:, 2048:T], in_=words_view(tab2_words, 0)[:, 2048:T])
        w1raw0 = load_weight(w1, 0, "w1raw0", "raw0")
        load_scales(w2s, w2_scales)
        l3 = load_list(offs3, "l3")
        s3 = load_scale_rows(tab3_scales, "s3", "s3")
        w1raw1 = load_weight(w1, 1, "w1raw1", "raw1")
        p2 = load_list(pos2, "p2")
        planes = [zeroed_plane(2 * S, "planes%d" % a) for a in range(2)]
        g1s = [plane[:, 0:S] for plane in planes]
        g3s = [plane[:, S : 2 * S] for plane in planes]
        w4s = zeroed_plane(H, "w4s")
        rows = tile([P, 2 * S], U8, "rows")

        nc.vector.tensor_copy(rows[:, 0:S], s1[:].indirect(l1[:]))
        t10 = load_table(tab_words, 0, "t10", "tabB")
        g2s = halves(gather_scales(s2, l2[:], "g2s"))
        w2d = tile([P, 2 * H], U8, "w2d")
        deal(w2d[:].bitcast(U16), w2raw[:].bitcast(U16))
        g2 = halves(gather_words(t2, l2[:], "g2"))
        w2sd = tile([P, H], U8, "w2sd")
        deal(w2sd[:], w2s[:])
        nc.vector.tensor_copy(rows[:, S : 2 * S], s3[:].indirect(l3[:]))
        place_scale_rows(rows, planes[0], 0)
        t11 = load_table(tab_words, 1, "t11", "tabC")
        place_scale_rows(rows, planes[1], 1)
        w1q = [quantise_weight(round_weight(w1raw0, "w1bf0", "bf0"), "w1q0", "s3")]
        w3raw0 = load_weight(w3, 0, "w3raw0", "raw0")
        p1 = load_list(pos1, "p1")
        t30 = load_table(tab3_words, 0, "t30", "tabA")

        bwin = [tile([P, S], F32, "bwin%d" % t) for t in range(4)]
        for t, h in by_slice:
            acc = bank(2 * t + h, "b%d%d" % (t, h))
            nc.tensor.matmul_mx(
                out=acc[:],
                lhsT=w2d[:, 2 * t * P : 2 * (t + 1) * P].bitcast(FP4X4),
                lhsT_scale=w2sd[:, t * P : (t + 1) * P],
                rhs=g2[h].bitcast(FP8X4),
                rhs_scale=g2s[h],
                start=True,
                stop=True,
            )
            nc.scalar.copy(out=bwin[t][:, h * N : (h + 1) * N], in_=acc[:])
        w1bf1 = round_weight(w1raw1, "w1bf1", "bf1")
        w3raw1 = load_weight(w3, 1, "w3raw1", "raw1")

        top = [tile([P, J], F32, "top%d" % t) for t in range(3)]
        for t in range(3):
            nc.vector.tensor_copy(top[t][:], bwin[t][:].indirect(p2[:]))

        g10 = halves(gather_words(t10, l1[:], "g10"))
        w1q.append(quantise_weight(w1bf1, "w1q1", "tabB"))
        g11 = [gather_words(t11, half(l1, h), "g11%d" % h)[:] for h in range(2)]
        top.append(tile([P, J], F32, "top3", "tabC"))
        nc.vector.tensor_copy(top[3][:], bwin[3][:].indirect(p2[:]))
        accs = {(t, h): bank(2 * t + h, "a%d%d" % (t, h)) for t, h in by_slice}
        mx_pass(accs, by_slice, w1q[0], g10, g1s, 0)
        mx_pass(accs, by_pair, w1q[1], g11, g1s, 1)
        t31 = load_table(tab3_words, 1, "t31", "tabB")
        load_scales(w4s, w4_scales)
        w4raw = tile([P, H], I32, "w4raw")
        nc.sync.dma_start(out=w4raw[:], in_=words_view(w4_words, 0))
        p3 = load_list(pos3, "p3")
        gain_sb = tile([P, 4], F32, "gain_sb")
        nc.sync.dma_start(out=gain_sb[:], in_=gain.rearrange("(p t) -> p t", t=4))
        awin = [tile([P, S], F32, "awin%d" % t) for t in range(4)]
        for t, h in by_pair:
            nc.scalar.copy(out=awin[t][:, h * N : (h + 1) * N], in_=accs[t, h][:])

        w4d = tile([P, H], I32, "w4d")
        deal(w4d[:], w4raw[:])
        w4sd = tile([P, H], U8, "w4sd")
        deal(w4sd[:], w4s[:])

        def pick_a(t, tag):
            ga = tile([P, J], F32, "ga%d" % t, tag)
            nc.vector.tensor_copy(ga[:], awin[t][:].indirect(p1[:]))
            return ga

        def larger_demand(t, ga, tag):
            larger = tile([P, J], F32, "larger%d" % t, tag)
            nc.vector.tensor_tensor(out=larger[:], in0=ga[:], in1=top[t][:], op=ALU.max)
            top[t] = larger

        ga = [pick_a(t, None) for t in range(3)]
        for t in range(3):
            larger_demand(t, ga[t], None)

        w3q = [quantise_weight(round_weight(w3raw0, "w3bf0", "bf0"), "w3q0", None)]
        g30 = halves(gather_words(t30, l3[:], "g30"))
        ga3 = pick_a(3, "tabA")
        w3bf1 = round_weight(w3raw1, "w3bf1", "bf1")
        accs = {(t, h): bank(2 * t + h, "d%d%d" % (t, h)) for t, h in by_slice}
        mx_pass(accs, by_slice, w3q[0], g30, g3s, 0)
        w3q.append(quantise_weight(w3bf1, "w3q1", None))
        g31 = [gather_words(t31, half(l3, h), "g31%d" % h)[:] for h in range(2)]
        larger_demand(3, ga3, "tabB")
        mx_pass(accs, by_pair, w3q[1], g31, g3s, 1)
        dwin = [tile([P, S], F32, "dwin%d" % t, "bwin%d" % t) for t in range(4)]
        for t, h in by_pair:
            nc.scalar.copy(out=dwin[t][:, h * N : (h + 1) * N], in_=accs[t, h][:])

        join = tile([P, 4, J], F32, "join")
        z = tile([P, 4, J], BF16, "z")
        HJ = J // 2
        for t, j0, j1 in [(0, 0, J), (1, 0, J), (2, 0, J), (3, 0, HJ), (3, HJ, J)]:
            neg = tile([P, j1 - j0], F32, "neg%d_%d" % (t, j0))
            nc.vector.tensor_tensor(
                out=neg[:], in0=dwin[t][:].indirect(p3[:, j0 // 16 : j1 // 16]), in1=top[t][:, j0:j1],
                op=ALU.subtract,
            )
            nc.scalar.activation(out=join[:, t, j0:j1], in_=neg[:], func=ACT.Tanh, scale=-1.0)
            if t == 0:
                nc.scalar.activation(
                    out=z[:, t, j0:j1], in_=join[:, t, j0:j1], func=ACT.Copy, scale=gain_sb[:, t : t + 1]
                )

        out_rows = out.rearrange("(p t) j -> p t j", t=4)
        quantised = []
        for h in range(2):
            for t in range(1, 4):
                cols = slice(h * HJ, (h + 1) * HJ)
                nc.vector.tensor_scalar(
                    out=z[:, t, cols], in0=join[:, t, cols], scalar1=gain_sb[:, t : t + 1], scalar2=None, op0=ALU.mult
                )
            zi = tile([P, HJ, 4], BF16, "zi%d" % h)
            weave = nc.vector.tensor_copy if h == 0 else nc.scalar.copy
            weave(
                zi[:].rearrange("p (c i) t -> p c t i", i=4),
                z[:, :, h * HJ : (h + 1) * HJ].rearrange("p t (c i) -> p c t i", i=4),
            )
            zq = tile([P, HJ], U32, "zq%d" % h)
            zs = tile([P, HJ], U8, "zs%d" % h)
            nc.vector.quantize_mx(
                out=zq[:].bitcast(FP8X4), scales=zs[:], in_=zi[:].rearrange("p j t -> p (j t)")
            )
            quantised.append((zq, zs))
        for h in range(2):
            cols = slice(h * HJ, (h + 1) * HJ)
            zq, zs = quantised[h]
            for u in range(2):
                res = tile([P, 2, HJ], F32, "res%d%d" % (h, u))
                for e in range(2):
                    t = 2 * u + e
                    acc = bank(4 * h + t, "y%d%d" % (h, t))
                    nc.tensor.matmul_mx(
                        out=acc[:, 0:HJ],
                        lhsT=fp8_cols(w4d, t),
                        lhsT_scale=w4sd[:, t * P : (t + 1) * P],
                        rhs=zq[:].bitcast(FP8X4),
                        rhs_scale=zs[:],
                        start=True,
                        stop=True,
                    )
                    nc.vector.tensor_tensor(out=res[:, e, :], in0=acc[:, 0:HJ], in1=join[:, t, cols], op=ALU.add)
                nc.sync.dma_start(out=out_rows[:, 2 * u : 2 * u + 2, cols], in_=res[:])
